import numpy as np
import ml_dtypes


def mxq(x, axis, fmt="e4m3"):
    dtype, down = {"e4m3": (ml_dtypes.float8_e4m3fn, 7), "e5m2": (ml_dtypes.float8_e5m2, 14)}[fmt]
    v = np.moveaxis(np.asarray(x, np.float32).astype(ml_dtypes.bfloat16).astype(np.float64), axis, -1)
    blocks = v.reshape(v.shape[:-1] + (-1, 32))
    amax = np.abs(blocks).max(-1, keepdims=True)
    byte = np.maximum(np.where(amax > 0, np.frexp(amax)[1] - 1 + 127, 0) - down, 1)
    scale = np.exp2(byte - 127.0)
    codes = (blocks / scale).astype(np.float32).astype(dtype).astype(np.float64)
    return np.moveaxis((codes * scale).reshape(v.shape), -1, axis)


WIDE = False


def mx_kscale(k):
    if not WIDE:
        return np.ones(k)
    levels = np.array([10, -10, 5, -5, 0])
    if k % 512:
        return np.exp2(np.random.permutation(np.resize(levels, k // 32))).repeat(32)
    a = np.empty((k // 512, 16))
    for p in range(k // 512):
        a[p, :8] = np.random.permutation(np.resize(levels, 8))
        for g in range(8):
            far = levels[np.abs(levels - a[p, g]) >= 10]
            a[p, g + 8] = far[np.random.randint(len(far))]
    return np.exp2(a.ravel()).repeat(32)


def f64(x):
    return np.asarray(x).astype(np.float64)


def striped8(idx):
    return np.asarray(idx).reshape(8, -1, 16).transpose(0, 2, 1).reshape(128, -1).astype(np.uint16)


def unstriped8(offs):
    return offs.reshape(8, 16, -1).transpose(0, 2, 1).reshape(8, -1).astype(np.int64)


def pick8(x, idx, run):
    r = np.arange(len(x))
    return x[r[:, None], idx[r % (8 * run) // run]]


E2M1 = np.array([0.0, 0.5, 1.0, 1.5, 2.0, 3.0, 4.0, 6.0, -0.0, -0.5, -1.0, -1.5, -2.0, -3.0, -4.0, -6.0])


def pack_weight(w, fmt):
    k, n = w.shape
    w = f64(np.asarray(w, np.float32).astype(ml_dtypes.bfloat16)).reshape(k // 32, 32, n)
    amax = np.abs(w).max(1)
    if fmt == "e4m3":
        byte = np.frexp(amax)[1] - 1 + 127 - 7
    else:
        mant, ex = np.frexp(amax / 6.0)
        byte = np.where(mant > 0.5, ex, ex - 1) + 127
    byte = np.clip(np.where(amax > 0, byte, 1), 1, 254)
    scaled = (w * np.exp2(127.0 - byte)[:, None, :]).reshape(k, n).astype(np.float32)
    by_word = np.ascontiguousarray(scaled.reshape(k // 512, 128, 4, n).transpose(0, 1, 3, 2))
    if fmt == "e4m3":
        words = by_word.astype(ml_dtypes.float8_e4m3fn).view(np.uint8)
    else:
        c = by_word.astype(ml_dtypes.float4_e2m1fn).view(np.uint8) & 0xF
        words = (c[..., 0::2] | (c[..., 1::2] << 4)).reshape(k // 512, 128, 2 * n)
    return np.ascontiguousarray(words), np.ascontiguousarray(byte.astype(np.uint8).reshape(k // 512, 16, n))


def unpack_weight(words, scales, fmt):
    g, _, n = scales.shape
    words = np.ascontiguousarray(words).reshape(g, 128, n, -1)
    if fmt == "e4m3":
        vals = words.view(ml_dtypes.float8_e4m3fn).astype(np.float64)
    else:
        nib = np.empty((g, 128, n, 4), np.uint8)
        nib[..., 0::2] = words & 0xF
        nib[..., 1::2] = words >> 4
        vals = E2M1[nib]
    vals = vals * np.repeat(np.exp2(scales.astype(np.float64) - 127.0), 8, axis=1)[..., None]
    return vals.transpose(0, 1, 3, 2).reshape(g * 512, n)


D, T, I, Q = 512, 1024, 512, 128


def setup_inputs():
    n = np.random.standard_normal
    idx = np.stack([np.random.permutation(T)[:I] for _ in range(8)])
    idx2 = np.stack([np.random.permutation(T)[:I] for _ in range(8)])
    idx3 = np.stack([np.random.permutation(T)[:I] for _ in range(8)])
    fd = mx_kscale(D)
    keysp = pack_weight(n((D, T)) / fd[:, None], "e4m3")
    return {
        "query": (n((D, Q)) * 1.0 / np.sqrt(D) * fd[:, None]).astype(np.float32),
        "keys_words": keysp[0],
        "keys_scales": keysp[1],
        "old": (1.0 * n((Q, T))).astype(np.float32),
        "offs": striped8(idx),
        "offs2": striped8(idx2),
        "offs3": striped8(idx3),
    }


def reference(query, keys_words, keys_scales, old, offs, offs2, offs3):
    idx = unstriped8(offs)
    idx2 = unstriped8(offs2)
    idx3 = unstriped8(offs3)
    keysu = unpack_weight(keys_words, keys_scales, "e4m3")
    queryq = mxq(f64(query), 0, "e4m3")
    a = queryq.T @ keysu
    w = pick8(a, idx, 16) * pick8(a, idx2, 16)
    f1 = np.zeros((Q, T))
    f1[np.arange(Q)[:, None], idx[np.arange(Q) % 128 // 16]] = w
    f2 = f1 + f64(old)
    y = pick8(f2, idx3, 16)
    return y

@@ -1,0 +1,104 @@
+from contextlib import ExitStack
+
+import concourse.mybir as mybir
+
+F32 = mybir.dt.float32
+BF16 = mybir.dt.bfloat16
+I32 = mybir.dt.int32
+U32 = mybir.dt.uint32
+U16 = mybir.dt.uint16
+U8 = mybir.dt.uint8
+FP8X4 = mybir.dt.float8_e4m3fn_x4
+COPY = mybir.ActivationFunctionType.Copy
+MULT = mybir.AluOpType.mult
+ADD = mybir.AluOpType.add
+
+D, T, SLOTS, Q = 512, 1024, 512, 128
+FLOPS = 2 * D * T * Q
+
+P = 128
+PACK = 4
+N_PASS = 256
+HALF = SLOTS // 2
+HALF_COLS = HALF // 16
+
+
+def tile_attend_pairproduct_lean_through_heads_kernel(
+    tc, query, keys_words, keys_scales, old, offs, offs2, offs3, out
+):
+    nc = tc.nc
+    with ExitStack() as ctx:
+        held = ctx.enter_context(tc.tile_pool(name="held", bufs=1))
+        psum = ctx.enter_context(tc.psum_pool(name="psum", bufs=1))
+
+        list1 = held.tile([P, SLOTS // 16], U16, name="list1")
+        list2 = held.tile([P, SLOTS // 16], U16, name="list2")
+        list3 = held.tile([P, SLOTS // 16], U16, name="list3")
+        q_raw = held.tile([P, PACK, Q], F32, name="q_raw")
+        q_bf = held.tile([P, Q, PACK], BF16, name="q_bf", align_bytes=64)
+        q_codes = held.tile([P, Q], U32, name="q_codes", align_bytes=64)
+        q_scales = held.tile([P, Q], U8, name="q_scales", align_bytes=64)
+        k_codes = [held.tile([P, T // 2], I32, name=f"k_codes{h}", align_bytes=64) for h in range(2)]
+        k_scales = held.tile([P, T], U8, name="k_scales", align_bytes=64)
+        scores = held.tile([P, T], F32, name="scores")
+        old_sb = held.tile([P, T], F32, name="old_sb")
+        placed = held.tile([P, T], F32, name="placed")
+        totals = held.tile([P, T], F32, name="totals")
+        first = [held.tile([P, HALF], F32, name=f"first{h}") for h in range(2)]
+        second = [held.tile([P, HALF], F32, name=f"second{h}") for h in range(2)]
+        picked = [held.tile([P, HALF], F32, name=f"picked{h}") for h in range(2)]
+
+        nc.vector.memset(placed[:], 0.0)
+
+        nc.sync.dma_start(out=q_raw[:], in_=query.rearrange("(p j) q -> p j q", j=PACK))
+        words = keys_words[0].rearrange("p t r -> p (t r)").bitcast(I32)
+        for h in range(2):
+            nc.sync.dma_start(out=k_codes[h][:], in_=words[:, h * (T // 2) : (h + 1) * (T // 2)])
+        scale_rows = keys_scales[0].bitcast(I32)
+        for quad in range(4):
+            nc.scalar.dma_start(
+                out=k_scales[32 * quad : 32 * quad + 4, :].bitcast(I32),
+                in_=scale_rows[4 * quad : 4 * quad + 4, :],
+            )
+        nc.sync.dma_start(list1[:], offs)
+        nc.sync.dma_start(list2[:], offs2)
+        nc.sync.dma_start(out=old_sb[:], in_=old)
+        nc.sync.dma_start(list3[:], offs3)
+
+        nc.vector.tensor_copy(out=q_bf[:], in_=q_raw[:].rearrange("p j q -> p q j"))
+        nc.vector.quantize_mx(
+            out=q_codes[:].bitcast(FP8X4), scales=q_scales[:], in_=q_bf[:].rearrange("p q j -> p (q j)")
+        )
+
+        for n in range(T // N_PASS):
+            cols = slice(n * N_PASS, (n + 1) * N_PASS)
+            half, start = divmod(n * N_PASS, T // 2)
+            bank = psum.tile([P, N_PASS], F32, name=f"bank{n}")
+            nc.tensor.matmul_mx(
+                out=bank[:],
+                lhsT=q_codes[:].bitcast(FP8X4),
+                lhsT_scale=q_scales[:],
+                rhs=k_codes[half][:, start : start + N_PASS].bitcast(FP8X4),
+                rhs_scale=k_scales[:, cols],
+                start=True,
+                stop=True,
+            )
+            if n % 2 == 0:
+                nc.scalar.activation(scores[:, cols], bank[:], COPY)
+            else:
+                nc.vector.tensor_copy(out=scores[:, cols], in_=bank[:])
+
+        halves = [slice(h * HALF_COLS, (h + 1) * HALF_COLS) for h in range(2)]
+        nc.vector.tensor_copy(first[0][:], scores[:].indirect(list1[:, halves[0]]))
+        nc.scalar.activation(second[0][:], scores[:].indirect(list2[:, halves[0]]), COPY)
+        nc.scalar.activation(first[1][:], scores[:].indirect(list1[:, halves[1]]), COPY)
+        nc.scalar.activation(second[1][:], scores[:].indirect(list2[:, halves[1]]), COPY)
+        for h in range(2):
+            nc.vector.tensor_tensor(placed[:].indirect(list1[:, halves[h]]), first[h][:], second[h][:], MULT)
+
+        nc.vector.tensor_tensor(totals[:], placed[:], old_sb[:], ADD)
+
+        nc.vector.tensor_copy(picked[0][:], totals[:].indirect(list3[:, halves[0]]))
+        nc.sync.dma_start(out=out[:, 0:HALF], in_=picked[0][:])
+        nc.scalar.activation(picked[1][:], totals[:].indirect(list3[:, halves[1]]), COPY)
+        nc.scalar.dma_start(out=out[:, HALF:SLOTS], in_=picked[1][:])

@@ -18,7 +18,8 @@ FLOPS = 2 * D * T * Q
 
 P = 128
 PACK = 4
-N_PASS = 256
+PASS_WIDTHS = (256, 256, 256, 128, 128)
+Q_VECTOR = 80
 HALF = SLOTS // 2
 HALF_COLS = HALF // 16
 
@@ -51,34 +52,43 @@ def tile_attend_pairproduct_lean_through_heads_kernel(
         nc.vector.memset(placed[:], 0.0)
 
         nc.sync.dma_start(out=q_raw[:], in_=query.rearrange("(p j) q -> p j q", j=PACK))
-        words = keys_words[0].rearrange("p t r -> p (t r)").bitcast(I32)
-        for h in range(2):
-            nc.sync.dma_start(out=k_codes[h][:], in_=words[:, h * (T // 2) : (h + 1) * (T // 2)])
         scale_rows = keys_scales[0].bitcast(I32)
         for quad in range(4):
-            nc.scalar.dma_start(
+            nc.sync.dma_start(
                 out=k_scales[32 * quad : 32 * quad + 4, :].bitcast(I32),
                 in_=scale_rows[4 * quad : 4 * quad + 4, :],
             )
+        words = keys_words[0].rearrange("p t r -> p (t r)").bitcast(I32)
+        for h in range(2):
+            nc.sync.dma_start(out=k_codes[h][:], in_=words[:, h * (T // 2) : (h + 1) * (T // 2)])
         nc.sync.dma_start(list1[:], offs)
         nc.sync.dma_start(list2[:], offs2)
         nc.sync.dma_start(out=old_sb[:], in_=old)
         nc.sync.dma_start(list3[:], offs3)
 
-        nc.vector.tensor_copy(out=q_bf[:], in_=q_raw[:].rearrange("p j q -> p q j"))
+        nc.vector.tensor_copy(
+            out=q_bf[:, :Q_VECTOR, :].rearrange("p (c i) j -> p c j i", i=4),
+            in_=q_raw[:, :, :Q_VECTOR].rearrange("p j (c i) -> p c j i", i=4),
+        )
+        nc.scalar.activation(
+            q_bf[:, Q_VECTOR:, :].rearrange("p (c i) j -> p c j i", i=4),
+            q_raw[:, :, Q_VECTOR:].rearrange("p j (c i) -> p c j i", i=4),
+            COPY,
+        )
         nc.vector.quantize_mx(
             out=q_codes[:].bitcast(FP8X4), scales=q_scales[:], in_=q_bf[:].rearrange("p q j -> p (q j)")
         )
 
-        for n in range(T // N_PASS):
-            cols = slice(n * N_PASS, (n + 1) * N_PASS)
-            half, start = divmod(n * N_PASS, T // 2)
-            bank = psum.tile([P, N_PASS], F32, name=f"bank{n}")
+        for n, width in enumerate(PASS_WIDTHS):
+            col0 = sum(PASS_WIDTHS[:n])
+            cols = slice(col0, col0 + width)
+            half, start = divmod(col0, T // 2)
+            bank = psum.tile([P, width], F32, name=f"bank{n}")
             nc.tensor.matmul_mx(
                 out=bank[:],
                 lhsT=q_codes[:].bitcast(FP8X4),
                 lhsT_scale=q_scales[:],
-                rhs=k_codes[half][:, start : start + N_PASS].bitcast(FP8X4),
+                rhs=k_codes[half][:, start : start + width].bitcast(FP8X4),
                 rhs_scale=k_scales[:, cols],
                 start=True,
                 stop=True,

@@ -19,7 +19,7 @@ FLOPS = 2 * D * T * Q
 P = 128
 PACK = 4
 PASS_WIDTHS = (256, 256, 256, 128, 128)
-Q_VECTOR = 80
+Q_VECTOR = 96
 HALF = SLOTS // 2
 HALF_COLS = HALF // 16
 
@@ -52,9 +52,10 @@ def tile_attend_pairproduct_lean_through_heads_kernel(
         nc.vector.memset(placed[:], 0.0)
 
         nc.sync.dma_start(out=q_raw[:], in_=query.rearrange("(p j) q -> p j q", j=PACK))
+        queues = (nc.sync, nc.scalar)
         scale_rows = keys_scales[0].bitcast(I32)
         for quad in range(4):
-            nc.sync.dma_start(
+            queues[quad // 2].dma_start(
                 out=k_scales[32 * quad : 32 * quad + 4, :].bitcast(I32),
                 in_=scale_rows[4 * quad : 4 * quad + 4, :],
             )
@@ -99,8 +100,8 @@ def tile_attend_pairproduct_lean_through_heads_kernel(
                 nc.vector.tensor_copy(out=scores[:, cols], in_=bank[:])
 
         halves = [slice(h * HALF_COLS, (h + 1) * HALF_COLS) for h in range(2)]
-        nc.vector.tensor_copy(first[0][:], scores[:].indirect(list1[:, halves[0]]))
-        nc.scalar.activation(second[0][:], scores[:].indirect(list2[:, halves[0]]), COPY)
+        nc.vector.tensor_copy(second[0][:], scores[:].indirect(list2[:, halves[0]]))
+        nc.scalar.activation(first[0][:], scores[:].indirect(list1[:, halves[0]]), COPY)
         nc.scalar.activation(first[1][:], scores[:].indirect(list1[:, halves[1]]), COPY)
         nc.scalar.activation(second[1][:], scores[:].indirect(list2[:, halves[1]]), COPY)
         for h in range(2):

from contextlib import ExitStack

import concourse.mybir as mybir

F32 = mybir.dt.float32
BF16 = mybir.dt.bfloat16
I32 = mybir.dt.int32
U32 = mybir.dt.uint32
U16 = mybir.dt.uint16
U8 = mybir.dt.uint8
FP8X4 = mybir.dt.float8_e4m3fn_x4
COPY = mybir.ActivationFunctionType.Copy
MULT = mybir.AluOpType.mult
ADD = mybir.AluOpType.add

D, T, SLOTS, Q = 512, 1024, 512, 128
FLOPS = 2 * D * T * Q

P = 128
PACK = 4
PASS_WIDTHS = (256, 256, 256, 128, 128)
Q_VECTOR = 96
HALF = SLOTS // 2
HALF_COLS = HALF // 16


def tile_attend_pairproduct_lean_through_heads_kernel(
    tc, query, keys_words, keys_scales, old, offs, offs2, offs3, out
):
    nc = tc.nc
    with ExitStack() as ctx:
        held = ctx.enter_context(tc.tile_pool(name="held", bufs=1))
        psum = ctx.enter_context(tc.psum_pool(name="psum", bufs=1))

        list1 = held.tile([P, SLOTS // 16], U16, name="list1")
        list2 = held.tile([P, SLOTS // 16], U16, name="list2")
        list3 = held.tile([P, SLOTS // 16], U16, name="list3")
        q_raw = held.tile([P, PACK, Q], F32, name="q_raw")
        q_bf = held.tile([P, Q, PACK], BF16, name="q_bf", align_bytes=64)
        q_codes = held.tile([P, Q], U32, name="q_codes", align_bytes=64)
        q_scales = held.tile([P, Q], U8, name="q_scales", align_bytes=64)
        k_codes = [held.tile([P, T // 2], I32, name=f"k_codes{h}", align_bytes=64) for h in range(2)]
        k_scales = held.tile([P, T], U8, name="k_scales", align_bytes=64)
        scores = held.tile([P, T], F32, name="scores")
        old_sb = held.tile([P, T], F32, name="old_sb")
        placed = held.tile([P, T], F32, name="placed")
        totals = held.tile([P, T], F32, name="totals")
        first = [held.tile([P, HALF], F32, name=f"first{h}") for h in range(2)]
        second = [held.tile([P, HALF], F32, name=f"second{h}") for h in range(2)]
        picked = [held.tile([P, HALF], F32, name=f"picked{h}") for h in range(2)]

        nc.vector.memset(placed[:], 0.0)

        nc.sync.dma_start(out=q_raw[:], in_=query.rearrange("(p j) q -> p j q", j=PACK))
        queues = (nc.sync, nc.scalar)
        scale_rows = keys_scales[0].bitcast(I32)
        for quad in range(4):
            queues[quad // 2].dma_start(
                out=k_scales[32 * quad : 32 * quad + 4, :].bitcast(I32),
                in_=scale_rows[4 * quad : 4 * quad + 4, :],
            )
        words = keys_words[0].rearrange("p t r -> p (t r)").bitcast(I32)
        for h in range(2):
            nc.sync.dma_start(out=k_codes[h][:], in_=words[:, h * (T // 2) : (h + 1) * (T // 2)])
        nc.sync.dma_start(list1[:], offs)
        nc.sync.dma_start(list2[:], offs2)
        nc.sync.dma_start(out=old_sb[:], in_=old)
        nc.sync.dma_start(list3[:], offs3)

        nc.vector.tensor_copy(
            out=q_bf[:, :Q_VECTOR, :].rearrange("p (c i) j -> p c j i", i=4),
            in_=q_raw[:, :, :Q_VECTOR].rearrange("p j (c i) -> p c j i", i=4),
        )
        nc.scalar.activation(
            q_bf[:, Q_VECTOR:, :].rearrange("p (c i) j -> p c j i", i=4),
            q_raw[:, :, Q_VECTOR:].rearrange("p j (c i) -> p c j i", i=4),
            COPY,
        )
        nc.vector.quantize_mx(
            out=q_codes[:].bitcast(FP8X4), scales=q_scales[:], in_=q_bf[:].rearrange("p q j -> p (q j)")
        )

        for n, width in enumerate(PASS_WIDTHS):
            col0 = sum(PASS_WIDTHS[:n])
            cols = slice(col0, col0 + width)
            half, start = divmod(col0, T // 2)
            bank = psum.tile([P, width], F32, name=f"bank{n}")
            nc.tensor.matmul_mx(
                out=bank[:],
                lhsT=q_codes[:].bitcast(FP8X4),
                lhsT_scale=q_scales[:],
                rhs=k_codes[half][:, start : start + width].bitcast(FP8X4),
                rhs_scale=k_scales[:, cols],
                start=True,
                stop=True,
            )
            if n % 2 == 0:
                nc.scalar.activation(scores[:, cols], bank[:], COPY)
            else:
                nc.vector.tensor_copy(out=scores[:, cols], in_=bank[:])

        halves = [slice(h * HALF_COLS, (h + 1) * HALF_COLS) for h in range(2)]
        nc.vector.tensor_copy(second[0][:], scores[:].indirect(list2[:, halves[0]]))
        nc.scalar.activation(first[0][:], scores[:].indirect(list1[:, halves[0]]), COPY)
        nc.scalar.activation(first[1][:], scores[:].indirect(list1[:, halves[1]]), COPY)
        nc.scalar.activation(second[1][:], scores[:].indirect(list2[:, halves[1]]), COPY)
        for h in range(2):
            nc.vector.tensor_tensor(placed[:].indirect(list1[:, halves[h]]), first[h][:], second[h][:], MULT)

        nc.vector.tensor_tensor(totals[:], placed[:], old_sb[:], ADD)

        nc.vector.tensor_copy(picked[0][:], totals[:].indirect(list3[:, halves[0]]))
        nc.sync.dma_start(out=out[:, 0:HALF], in_=picked[0][:])
        nc.scalar.activation(picked[1][:], totals[:].indirect(list3[:, halves[1]]), COPY)
        nc.scalar.dma_start(out=out[:, HALF:SLOTS], in_=picked[1][:])
